import numpy as np, ml_dtypes
CORES = [73,201,329,457,330]
N = 5
import mx_ref
NC = 128
BF = ml_dtypes.bfloat16
def cut(t, i, w=512):
    return t[:, w * i:w * i + w]
def tile(rs):
    return np.stack(rs, axis=2).reshape(128, -1).astype(BF)
def onehot(t, r):
    own, p, b = t[:, :NC], t[:, NC:2 * NC], t[:, 2 * NC:]
    return tile([((own == r) & (p == np.arange(128)[:, None]) & (b == f)).astype(np.float32) for f in range(4)])
def setup_inputs(rng):
    def f(*shape):
        return mx_ref.flush((rng.standard_normal(shape, dtype=np.float32) * np.exp2(rng.integers(-2, 3, shape[:-1] + (1,)))).astype(BF))
    t = np.concatenate([rng.integers(0, N, (N, 1, NC)), rng.integers(0, 128, (N, 1, NC)), rng.integers(0, 4, (N, 1, NC))], axis=2)
    return {"tg": np.broadcast_to(t, (N, 128, 3 * NC)).astype(BF).copy(), "tab": f(N, 128, 4 * 512), "w": f(N, 128, 512)}
def setup_inputs_blocks(rng):
    d = setup_inputs(rng)
    for k in ("tab", "w"): d[k] = mx_ref.spread(d[k], rng, 4)
    return d
def setup_inputs_wide(rng):
    d = setup_inputs(rng)
    for k in ("tab", "w"): d[k] = mx_ref.flush((d[k].astype(np.float32) * np.exp2(rng.integers(-6, 7, (N, 1, 1))).astype(np.float32)).astype(BF))
    return d
def setup_inputs_hot(rng):
    d = setup_inputs(rng); t = d["tg"].astype(np.float32); t[:, :, :NC] = rng.integers(0, N); t[:, :, NC:2 * NC] = np.broadcast_to(rng.integers(0, 4, (N, 1, NC)), (N, 128, NC))
    d["tg"] = t.astype(BF)
    return d
def reference(tg, tab, w):
    y = np.zeros((N, 128, NC), np.float32)
    for j in range(N):
        qw = mx_ref.quantize(w[j])
        for r in range(N):
            o = mx_ref.quantize(onehot(tg[j].astype(np.float32), r))
            e = mx_ref.quantize(tile([mx_ref.matmul(mx_ref.quantize(cut(tab[r], f)), o) for f in range(4)]))
            p = mx_ref.matmul(qw, e)
            y[j] = p if r == 0 else y[j] + p
    return {"y": y}

@@ -1,0 +1,300 @@
+import math
+from concourse.bass import DstId, RemoteDMATransfer
+from concourse.mybir import dt, AluOpType, ActivationFunctionType
+
+N = 5
+POS = {0: 0, 1: 1, 3: 2, 2: 3, 4: 4}
+GROUPS = {0: [[0], [1], [2, 4], [3]],
+          1: [[1], [0], [3], [2, 4]],
+          2: [[2], [3], [0], [4, 1]],
+          3: [[3], [2, 4], [1], [0]],
+          4: [[4], [1], [0], [2, 3]]}
+KEY_CALLS = {0: [[1], [3]], 1: [[4], [0, 2]], 2: [[3], [4, 1]], 3: [[2], [0, 4]], 4: [[3], [2, 1]]}
+KEY_RELAY = {1: ([0], [2, 4]), 3: ([2, 4], [0]), 4: ([1], [3]), 2: ([3], [1])}
+DIAG = {(0, 2), (0, 4), (2, 0), (4, 0), (1, 3), (3, 1)}
+
+SCRATCH = {
+    "tgs": ("sbuf", [128, 384], "bfloat16"),
+    "tgt": ("sbuf", [128, 384], "bfloat16"),
+    "tabs": ("sbuf", [128, 2048], "bfloat16"),
+    "ws": ("sbuf", [128, 512], "bfloat16"),
+    "kp": ("sbuf", [128, 1], "float32"),
+    "ex": ("sbuf", [128, 4], "float32"),
+    "e4": ("sbuf", [128, 4], "bfloat16"),
+    "kc": ("sbuf", [128, 4], "float32"),
+    "ones": ("sbuf", [128, 32], "bfloat16"),
+    "g1": ("sbuf", [128, 4], "bfloat16"),
+    "g2": ("sbuf", [128, 4], "bfloat16"),
+    "p1": ("sbuf", [128, 4], "float32"),
+    "m1": ("sbuf", [128, 4], "float32"),
+    "key": ("sbuf", [128, 2], "bfloat16"),
+    "kl": ("sbuf", [128, 2 * N], "bfloat16"),
+    "sp": ("sbuf", [128, 64 * N], "bfloat16"),
+    "rows": ("sbuf", [128, 128 * N], "bfloat16"),
+    "ot": ("sbuf", [128, 512 * N], "bfloat16"),
+    "et": ("sbuf", [128, 512 * N], "bfloat16"),
+    "tq": ("sbuf", [128, 512], "float8_e4m3fn_x4"),
+    "tqs": ("sbuf", [128, 512], "uint8"),
+    "wq": ("sbuf", [128, 128], "float8_e4m3fn_x4"),
+    "wqs": ("sbuf", [128, 128], "uint8"),
+    "oc": ("sbuf", [128, 128 * N], "float8_e4m3fn_x4"),
+    "osc": ("sbuf", [128, 128 * N], "uint8"),
+    "xc": ("sbuf", [128, 128 * N], "float8_e4m3fn_x4"),
+    "xsc": ("sbuf", [128, 128 * N], "uint8"),
+    "ec": ("sbuf", [128, 128 * N], "float8_e4m3fn_x4"),
+    "esc": ("sbuf", [128, 128 * N], "uint8"),
+    "z": ("psum", [128, 4096], "float32"),
+    "ysb": ("sbuf", [128, 128], "float32"),
+}
+SEMAPHORES = (["ltg", "ltab", "lw", "iot", "e4d", "kcd", "one", "tt", "gg1", "gg2", "pp1", "mm1", "keyd", "tqd", "wqd",
+               "yd", "yc", "yst", "sent"]
+              + ["%s%d" % (n, q) for q in range(4) for n in ("x", "r", "o", "q", "z0", "z1", "z2", "z3", "c", "e")]
+              + ["%s%d" % (n, r) for r in range(N) for n in ("kin", "cin", "sin")])
+
+
+def helpers(T, topo):
+    def around(rank):
+        me = T.cores[rank]
+        on = [c for c in range(512) if topo.host(c) == topo.host(me) and topo.chip(c) == topo.chip(me) and c not in T.cores]
+        return [c for c in on if topo.die(c) == topo.die(me)], [c for c in on if topo.die(c) != topo.die(me)]
+    n1, f1 = around(1)
+    n0, f0 = around(0)
+    return {"c02": n1[2], "c04": f1[0], "s0": f1[2], "c20": f1[1], "c40": f1[3], "s24": n1[1],
+            "c13": n0[2], "s1": f0[0], "c31": f0[2], "s3": f0[3]}
+
+
+def rank_program(g, core, T, topo):
+    rank = T.rank_of(core)
+    H = helpers(T, topo)
+    R = T.cores
+    sem = T.sem
+    sent = [0]
+
+    def codes(t, i, n=1):
+        return t[:, 128 * i:128 * (i + n)].bitcast(dt.uint8)
+
+    def planes(t, i, n=1):
+        return t[:, 128 * i:128 * (i + n)]
+
+    def parts(dsts, k):
+        m = topo.mask(core, dsts[0])
+        for d in dsts:
+            m &= topo.mask(core, d)
+        low = [e for e in range(16) if m >> e & 1][:8]
+        w = 8 // k
+        return [sum(1 << e for e in low[w * i:w * i + w]) for i in range(k)], w
+
+    def send(moves):
+        masks, w = parts([m[0] for m in moves], len(moves))
+        if len(moves) == 1:
+            d, out, src, s = moves[0]
+            rid, pid = topo.addr(d, core)
+            g.remote_dma(out, src, s, sem.sent, pid, rid, masks[0])
+        else:
+            tr = []
+            for (d, out, src, s), m in zip(moves, masks):
+                rid, pid = topo.addr(d, core)
+                tr.append(RemoteDMATransfer(dst_ids=[DstId(rid=rid, pnc=pid)], dma_engine_mask=m, remote_sem=s, src=src, dst=out))
+            g.remote_dma_fused(tr, local_sem=sem.sent)
+        sent[0] += w * len(moves)
+
+    def spread(dsts, out, src, s):
+        if len(dsts) == 1:
+            return send([(dsts[0], out, src, s)])
+        masks, w = parts(dsts, 1)
+        ids = []
+        for d in dsts:
+            rid, pid = topo.addr(d, core)
+            ids.append(DstId(rid=rid, pnc=pid))
+        g.remote_dma_fused([RemoteDMATransfer(dst_ids=ids, dma_engine_mask=masks[0], remote_sem=s, srcs=[src],
+                                              dsts=[out for _ in dsts])], local_sem=sem.sent)
+        sent[0] += w
+
+    def fan(r, j):
+        for q in GROUPS[r]:
+            if j in q:
+                return 8 // len(q)
+
+    if rank is None:
+        names = [n for n in H if H[n] == core]
+        if not names:
+            return
+        name = names[0]
+        if name in ("c02", "c04", "c20", "c40", "c13", "c31"):
+            r, j = int(name[1]), int(name[2])
+            g.wait_ge(sem["cin%d" % r], fan(r, j))
+            send([(R[j], codes(T.ec, POS[r]), codes(T.ec, POS[r]), sem["cin%d" % r])])
+        elif name == "s0":
+            g.wait_ge(sem.sin0, 8)
+            send([(R[2], planes(T.esc, POS[0]), planes(T.esc, 0), sem.sin0),
+                  (R[4], planes(T.esc, POS[0]), planes(T.esc, 1), sem.sin0)])
+        elif name == "s24":
+            g.wait_ge(sem.sin2, 8)
+            g.wait_ge(sem.sin4, 8)
+            send([(R[0], planes(T.esc, POS[2], 2), planes(T.esc, POS[2], 2), sem.sin2)])
+        else:
+            r = int(name[1])
+            g.wait_ge(sem["sin%d" % r], 8)
+            send([(R[4 - r], planes(T.esc, POS[r]), planes(T.esc, POS[r]), sem["sin%d" % r])])
+        g.wait_ge(sem.sent, sent[0])
+        return
+
+    V, S, E, Y = g.vector, g.scalar, g.tensor, g.sync
+    EQ, MUL, ADD = AluOpType.is_equal, AluOpType.mult, AluOpType.add
+    EXP, COPY = ActivationFunctionType.Exp, ActivationFunctionType.Copy
+    LN2 = math.log(2.0)
+    groups = GROUPS[rank]
+    first = [0]
+    for q in groups:
+        first.append(first[-1] + len(q))
+
+    Y.dma_start(T.tgs[:], T.tg[:, :]).then_inc(sem.ltg, 16)
+    Y.dma_start(T.tabs[:], T.tab[:, :]).then_inc(sem.ltab, 16)
+    Y.dma_start(T.ws[:], T.w[:, :]).then_inc(sem.lw, 16)
+
+    g.iota(T.ex[:], [[1, 4]], 4 * rank, 0, allow_small_or_imprecise_dtypes=True).then_inc(sem.iot, 1)
+    g.iota(T.kp[:], [[1, 1]], 128, 1, allow_small_or_imprecise_dtypes=True).then_inc(sem.iot, 1)
+    S.wait_ge(sem.iot, 2)
+    S.activation(T.e4[:], T.ex[:], EXP, scale=LN2).then_inc(sem.e4d, 1)
+    V.memset(T.ones[:], 1.0).then_inc(sem.one, 1)
+    V.wait_ge(sem.iot, 2)
+    V.wait_ge(sem.e4d, 1)
+    V.tensor_scalar(T.kc[:], T.e4[:], T.kp[:, 0:1], None, MUL).then_inc(sem.kcd, 1)
+
+    V.wait_ge(sem.ltg, 16)
+    V.transpose(T.tgt[:], T.tgs[:]).then_inc(sem.tt, 1)
+    S.wait_ge(sem.tt, 1)
+    S.activation(T.g1[:], T.tgt[:, 0:128:32], EXP, scale=4 * LN2).then_inc(sem.gg1, 1)
+    S.activation(T.g2[:], T.tgt[:, 256:384:32], EXP, scale=LN2).then_inc(sem.gg2, 1)
+    V.wait_ge(sem.tt, 1)
+    V.tensor_scalar(T.p1[:], T.tgt[:, 128:256:32], 128.0, None, ADD).then_inc(sem.pp1, 1)
+    V.wait_ge(sem.pp1, 1)
+    V.wait_ge(sem.gg1, 1)
+    V.tensor_tensor(T.m1[:], T.p1[:], T.g1[:], MUL).then_inc(sem.mm1, 1)
+    V.wait_ge(sem.mm1, 1)
+    V.wait_ge(sem.gg2, 1)
+    V.tensor_tensor(T.key[0:64, 0:2], T.m1[0:64, 0:2], T.g2[0:64, 0:2], MUL).then_inc(sem.keyd, 1)
+    V.tensor_tensor(T.key[64:128, 0:2], T.m1[64:128, 2:4], T.g2[64:128, 2:4], MUL).then_inc(sem.keyd, 1)
+
+    g.wait_ge(sem.keyd, 2)
+    lo = 2 * POS[rank]
+    for dsts in KEY_CALLS[rank]:
+        spread([R[d] for d in dsts], T.kl[:, lo:lo + 2], T.key[:, 0:2], sem["kin%d" % rank])
+    if rank in KEY_RELAY:
+        srcs, dsts = KEY_RELAY[rank]
+        for s in srcs:
+            g.wait_ge(sem["kin%d" % s], 8)
+        lo, hi = 2 * POS[srcs[0]], 2 * POS[srcs[-1]] + 2
+        spread([R[d] for d in dsts], T.kl[:, lo:hi], T.kl[:, lo:hi], sem["kin%d" % srcs[0]])
+
+    def make_o(q):
+        for n, j in enumerate(groups[q]):
+            i = first[q] + n
+            if j == rank:
+                V.wait_ge(sem.keyd, 2)
+                V.wait_ge(sem.one, 1)
+                V.wait_ge(sem.kcd, 1)
+                src, c0 = T.key, 0
+            else:
+                s = 2 if (rank == 0 and j == 4) else j
+                V.wait_ge(sem["kin%d" % s], 8)
+                src, c0 = T.kl, 2 * POS[j]
+            for k in range(2):
+                V.tensor_scalar(T.sp[:, 64 * i + 32 * k:64 * i + 32 * k + 32], T.ones[:], src[:, c0 + k:c0 + k + 1], None,
+                                MUL).then_inc(sem["x%d" % q], 1)
+        V.wait_ge(sem["x%d" % q], 2 * len(groups[q]))
+        for n in range(len(groups[q])):
+            i = first[q] + n
+            for h in range(2):
+                for to in range(2):
+                    V.transpose(T.rows[64 * to:64 * to + 64, 128 * i + 64 * h:128 * i + 64 * h + 64],
+                                T.sp[64 * h:64 * h + 64, 64 * i:64 * i + 64]).then_inc(sem["r%d" % q], 1)
+        V.wait_ge(sem["r%d" % q], 4 * len(groups[q]))
+        a, b = 128 * first[q], 128 * first[q + 1]
+        for f in range(4):
+            V.tensor_scalar(T.ot[:, 4 * a + f:4 * b:4], T.rows[:, a:b], T.kc[:, f:f + 1], None, EQ).then_inc(sem["o%d" % q], 1)
+        V.wait_ge(sem["o%d" % q], 4)
+        V.quantize_mx(T.oc[:, a:b], T.osc[:, a:b], T.ot[:, 4 * a:4 * b]).then_inc(sem["q%d" % q], 1)
+
+    def make_z(q):
+        a, b = 128 * first[q], 128 * first[q + 1]
+        E.wait_ge(sem["q%d" % q], 1)
+        if q == 0:
+            E.wait_ge(sem.tqd, 4)
+        if q >= 2:
+            E.wait_ge(sem["c%d" % (q - 2)], 4)
+        for f in range(4):
+            c = 512 * (f + 4 * (q % 2))
+            E.matmul_mx(T.z[:, c:c + b - a], T.tq[:, 128 * f:128 * f + 128], T.tqs[:, 128 * f:128 * f + 128],
+                        T.oc[:, a:b], T.osc[:, a:b], True, True).then_inc(sem["z%d%d" % (f, q)], 1)
+
+    def make_e(q):
+        a, b = 128 * first[q], 128 * first[q + 1]
+        for f in range(4):
+            c = 512 * (f + 4 * (q % 2))
+            out, src = T.et[:, 4 * a + f:4 * b:4], T.z[:, c:c + b - a]
+            if f % 2 == 0:
+                V.wait_ge(sem["z%d%d" % (f, q)], 1)
+                V.tensor_copy(out, src).then_inc(sem["c%d" % q], 1)
+            else:
+                S.wait_ge(sem["z%d%d" % (f, q)], 1)
+                S.activation(out, src, COPY).then_inc(sem["c%d" % q], 1)
+        V.wait_ge(sem["c%d" % q], 4)
+        V.quantize_mx(T.xc[:, a:b], T.xsc[:, a:b], T.et[:, 4 * a:4 * b]).then_inc(sem["e%d" % q], 1)
+
+    make_o(0)
+    V.wait_ge(sem.ltab, 16)
+    for f in range(4):
+        V.quantize_mx(T.tq[:, 128 * f:128 * f + 128], T.tqs[:, 128 * f:128 * f + 128],
+                      T.tabs[:, 512 * f:512 * f + 512]).then_inc(sem.tqd, 1)
+    V.wait_ge(sem.lw, 16)
+    V.quantize_mx(T.wq[:], T.wqs[:], T.ws[:]).then_inc(sem.wqd, 1)
+    make_z(0)
+    make_e(0)
+    for q in (1, 2, 3):
+        make_o(q)
+        make_z(q)
+        make_e(q)
+
+    for q in (1, 2, 3):
+        g.wait_ge(sem["e%d" % q], 1)
+        i0, dst = first[q], groups[q]
+        if (rank, dst[0]) in DIAG:
+            cs, ss = sem["cin%d" % rank], sem["sin%d" % rank]
+            send([(H["c%d%d" % (rank, j)], codes(T.ec, POS[rank]), codes(T.xc, i0 + n), cs) for n, j in enumerate(dst)])
+            if rank == 0:
+                send([(H["s0"], planes(T.esc, 0, 2), planes(T.xsc, i0, 2), ss)])
+            else:
+                hs = H["s24"] if rank in (2, 4) else H["s%d" % rank]
+                send([(hs, planes(T.esc, POS[rank]), planes(T.xsc, i0), ss)])
+        else:
+            send([(R[j], codes(T.ec, POS[rank]), codes(T.xc, i0 + n), sem["cin%d" % rank]) for n, j in enumerate(dst)])
+            send([(R[j], planes(T.esc, POS[rank]), planes(T.xsc, i0 + n), sem["sin%d" % rank]) for n, j in enumerate(dst)])
+
+    E.wait_ge(sem.wqd, 1)
+    E.wait_ge(sem.e0, 1)
+    E.wait_ge(sem.c2, 4)
+    far = [r for r in range(N) if (r, rank) in DIAG]
+    near = [r for r in range(N) if r != rank and r not in far]
+    E.matmul_mx(T.z[:, 0:128], T.wq[:], T.wqs[:], T.xc[:, 0:128], T.xsc[:, 0:128], True, False)
+    todo = near + far
+    for r in todo:
+        p = 128 * POS[r]
+        direct = r in near
+        E.wait_ge(sem["cin%d" % r], fan(r, rank) if direct else 8)
+        if direct:
+            E.wait_ge(sem["sin%d" % r], fan(r, rank))
+        elif r == 0:
+            E.wait_ge(sem.sin0, 4)
+        else:
+            E.wait_ge(sem["sin%d" % (2 if rank == 0 else r)], 8)
+        last = r == todo[-1]
+        m = E.matmul_mx(T.z[:, 0:128], T.wq[:], T.wqs[:], T.ec[:, p:p + 128], T.esc[:, p:p + 128], False, last)
+        if last:
+            m.then_inc(sem.yd, 1)
+    V.wait_ge(sem.yd, 1)
+    V.tensor_copy(T.ysb[:], T.z[:, 0:128]).then_inc(sem.yc, 1)
+    Y.wait_ge(sem.yc, 1)
+    Y.dma_start(T.y[:, :], T.ysb[:]).then_inc(sem.yst, 16)
+    Y.wait_ge(sem.yst, 16)
+    g.wait_ge(sem.sent, sent[0])

@@ -4,51 +4,36 @@ from concourse.mybir import dt, AluOpType, ActivationFunctionType
 
 N = 5
 POS = {0: 0, 1: 1, 3: 2, 2: 3, 4: 4}
-GROUPS = {0: [[0], [1], [2, 4], [3]],
-          1: [[1], [0], [3], [2, 4]],
+GROUPS = {0: [[0], [1], [2], [4], [3]],
+          1: [[1], [0], [2], [3], [4]],
           2: [[2], [3], [0], [4, 1]],
-          3: [[3], [2, 4], [1], [0]],
+          3: [[3], [2], [4], [1], [0]],
           4: [[4], [1], [0], [2, 3]]}
-KEY_CALLS = {0: [[1], [3]], 1: [[4], [0, 2]], 2: [[3], [4, 1]], 3: [[2], [0, 4]], 4: [[3], [2, 1]]}
+VSEQ = {0: ["e0", "o1", "e1", "o2", "o3", "e2", "e3", "o4", "e4"],
+        1: ["e0", "o1", "o2", "e1", "e2", "o3", "e3", "o4", "e4"],
+        2: ["e0", "o1", "e1", "o2", "e2", "o3", "e3"],
+        3: ["e0", "o1", "o2", "e1", "e2", "o3", "e3", "o4", "e4"],
+        4: ["e0", "o1", "e1", "o2", "e2", "o3", "e3"]}
+VCOPY = {r: [0, 1, 2, 3, 4] for r in range(N)}
+SEND = {0: ["C1", "S1", "C2", "S24", "C4", "C3", "S3"],
+        1: ["C0", "S0", "C2", "S2", "C3", "S3", "C4", "S4"],
+        2: ["C3", "S3", "C0", "S0", "C41", "S41"],
+        3: ["C2", "S2", "C4", "S4", "C1", "S1", "C0", "S0"],
+        4: ["C1", "S1", "C0", "S0", "C23", "S23"]}
+KEY_CALLS = {0: [[1], [3]], 1: [[4], [0], [2]], 2: [[3], [4, 1]], 3: [[2], [0], [4]], 4: [[3], [2, 1]]}
 KEY_RELAY = {1: ([0], [2, 4]), 3: ([2, 4], [0]), 4: ([1], [3]), 2: ([3], [1])}
 DIAG = {(0, 2), (0, 4), (2, 0), (4, 0), (1, 3), (3, 1)}
-
-SCRATCH = {
-    "tgs": ("sbuf", [128, 384], "bfloat16"),
-    "tgt": ("sbuf", [128, 384], "bfloat16"),
-    "tabs": ("sbuf", [128, 2048], "bfloat16"),
-    "ws": ("sbuf", [128, 512], "bfloat16"),
-    "kp": ("sbuf", [128, 1], "float32"),
-    "ex": ("sbuf", [128, 4], "float32"),
-    "e4": ("sbuf", [128, 4], "bfloat16"),
-    "kc": ("sbuf", [128, 4], "float32"),
-    "ones": ("sbuf", [128, 32], "bfloat16"),
-    "g1": ("sbuf", [128, 4], "bfloat16"),
-    "g2": ("sbuf", [128, 4], "bfloat16"),
-    "p1": ("sbuf", [128, 4], "float32"),
-    "m1": ("sbuf", [128, 4], "float32"),
-    "key": ("sbuf", [128, 2], "bfloat16"),
-    "kl": ("sbuf", [128, 2 * N], "bfloat16"),
-    "sp": ("sbuf", [128, 64 * N], "bfloat16"),
-    "rows": ("sbuf", [128, 128 * N], "bfloat16"),
-    "ot": ("sbuf", [128, 512 * N], "bfloat16"),
-    "et": ("sbuf", [128, 512 * N], "bfloat16"),
-    "tq": ("sbuf", [128, 512], "float8_e4m3fn_x4"),
-    "tqs": ("sbuf", [128, 512], "uint8"),
-    "wq": ("sbuf", [128, 128], "float8_e4m3fn_x4"),
-    "wqs": ("sbuf", [128, 128], "uint8"),
-    "oc": ("sbuf", [128, 128 * N], "float8_e4m3fn_x4"),
-    "osc": ("sbuf", [128, 128 * N], "uint8"),
-    "xc": ("sbuf", [128, 128 * N], "float8_e4m3fn_x4"),
-    "xsc": ("sbuf", [128, 128 * N], "uint8"),
-    "ec": ("sbuf", [128, 128 * N], "float8_e4m3fn_x4"),
-    "esc": ("sbuf", [128, 128 * N], "uint8"),
-    "z": ("psum", [128, 4096], "float32"),
-    "ysb": ("sbuf", [128, 128], "float32"),
-}
+BF, F32, MX, U8 = "bfloat16", "float32", "float8_e4m3fn_x4", "uint8"
+SCRATCH = {n: ("sbuf", [128, w], d) for n, w, d in (
+    ("tgs", 384, BF), ("tgt", 384, BF), ("tabs", 2048, BF), ("ws", 512, BF), ("kp", 1, F32), ("ex", 4, F32), ("e4", 4, BF),
+    ("kc", 4, F32), ("ones", 32, BF), ("g1", 4, BF), ("g2", 4, BF), ("p1", 4, F32), ("m1", 4, F32), ("key", 2, BF),
+    ("kl", 2 * N, BF), ("sp", 64 * N, BF), ("rows", 128 * N, BF), ("ot", 512 * N, BF), ("et", 512 * N, BF),
+    ("tq", 512, MX), ("tqs", 512, U8), ("wq", 128, MX), ("wqs", 128, U8), ("oc", 128 * N, MX), ("osc", 128 * N, U8),
+    ("xc", 128 * N, MX), ("xsc", 128 * N, U8), ("ec", 128 * N, MX), ("esc", 128 * N, U8), ("ysb", 128, F32))}
+SCRATCH["z"] = ("psum", [128, 4096], F32)
 SEMAPHORES = (["ltg", "ltab", "lw", "iot", "e4d", "kcd", "one", "tt", "gg1", "gg2", "pp1", "mm1", "keyd", "tqd", "wqd",
                "yd", "yc", "yst", "sent"]
-              + ["%s%d" % (n, q) for q in range(4) for n in ("x", "r", "o", "q", "z0", "z1", "z2", "z3", "c", "e")]
+              + ["%s%d" % (n, q) for q in range(5) for n in ("x", "r", "o", "q", "z0", "z1", "z2", "z3", "c", "e")]
               + ["%s%d" % (n, r) for r in range(N) for n in ("kin", "cin", "sin")])
 
 
@@ -76,53 +61,60 @@ def rank_program(g, core, T, topo):
     def planes(t, i, n=1):
         return t[:, 128 * i:128 * (i + n)]
 
-    def parts(dsts, k):
-        m = topo.mask(core, dsts[0])
-        for d in dsts:
-            m &= topo.mask(core, d)
-        low = [e for e in range(16) if m >> e & 1][:8]
-        w = 8 // k
-        return [sum(1 << e for e in low[w * i:w * i + w]) for i in range(k)], w
+    def bits(m):
+        return [e for e in range(16) if m >> e & 1]
+
+    def here(c, d):
+        return (topo.host(d), topo.chip(d)) == (topo.host(c), topo.chip(c))
+
+    def masks(c, dsts):
+        leave = [topo.mask(c, d) for d in R if topo.may_write(c, d) and not here(c, d)][0]
+        on = [here(c, d) for d in dsts]
+        lists = []
+        for i, d in enumerate(dsts):
+            pool = bits(topo.mask(c, d) & ~leave) if on[i] else bits(topo.mask(c, d))
+            k, w = on[:i].count(on[i]), len(pool) // on.count(on[i])
+            lists.append(pool[k * w:k * w + w])
+        return lists
 
     def send(moves):
-        masks, w = parts([m[0] for m in moves], len(moves))
+        es = masks(core, [m[0] for m in moves])
         if len(moves) == 1:
             d, out, src, s = moves[0]
             rid, pid = topo.addr(d, core)
-            g.remote_dma(out, src, s, sem.sent, pid, rid, masks[0])
+            g.remote_dma(out, src, s, sem.sent, pid, rid, sum(1 << e for e in es[0]))
         else:
             tr = []
-            for (d, out, src, s), m in zip(moves, masks):
+            for (d, out, src, s), l in zip(moves, es):
                 rid, pid = topo.addr(d, core)
-                tr.append(RemoteDMATransfer(dst_ids=[DstId(rid=rid, pnc=pid)], dma_engine_mask=m, remote_sem=s, src=src, dst=out))
+                tr.append(RemoteDMATransfer(dst_ids=[DstId(rid=rid, pnc=pid)], dma_engine_mask=sum(1 << e for e in l),
+                                            remote_sem=s, src=src, dst=out))
             g.remote_dma_fused(tr, local_sem=sem.sent)
-        sent[0] += w * len(moves)
+        sent[0] += sum(len(l) for l in es)
 
-    def spread(dsts, out, src, s):
-        if len(dsts) == 1:
-            return send([(dsts[0], out, src, s)])
-        masks, w = parts(dsts, 1)
-        ids = []
-        for d in dsts:
-            rid, pid = topo.addr(d, core)
-            ids.append(DstId(rid=rid, pnc=pid))
-        g.remote_dma_fused([RemoteDMATransfer(dst_ids=ids, dma_engine_mask=masks[0], remote_sem=s, srcs=[src],
-                                              dsts=[out for _ in dsts])], local_sem=sem.sent)
-        sent[0] += w
-
-    def fan(r, j):
-        for q in GROUPS[r]:
+    def count(r, j, calls):
+        for q in calls:
             if j in q:
-                return 8 // len(q)
+                to = [H["c%d%d" % (r, d)] if (r, d) in DIAG else R[d] for d in q]
+                return len(masks(R[r], to)[q.index(j)])
+
+    def fan(r, j, kind):
+        return count(r, j, [[int(d) for d in s[1:]] for s in SEND[r] if s[0] == kind])
+
+    def keys_in(s, j):
+        if (s, j) in DIAG:
+            via = [v for v in KEY_RELAY if s in KEY_RELAY[v][0] and j in KEY_RELAY[v][1]][0]
+            return count(via, j, [KEY_RELAY[via][1]])
+        return count(s, j, KEY_CALLS[s])
 
     if rank is None:
         names = [n for n in H if H[n] == core]
         if not names:
             return
         name = names[0]
-        if name in ("c02", "c04", "c20", "c40", "c13", "c31"):
+        if name[0] == "c":
             r, j = int(name[1]), int(name[2])
-            g.wait_ge(sem["cin%d" % r], fan(r, j))
+            g.wait_ge(sem["cin%d" % r], fan(r, j, "C"))
             send([(R[j], codes(T.ec, POS[r]), codes(T.ec, POS[r]), sem["cin%d" % r])])
         elif name == "s0":
             g.wait_ge(sem.sin0, 8)
@@ -147,6 +139,7 @@ def rank_program(g, core, T, topo):
     first = [0]
     for q in groups:
         first.append(first[-1] + len(q))
+    slot = {j: i for i, j in enumerate([j for q in groups for j in q])}
 
     Y.dma_start(T.tgs[:], T.tg[:, :]).then_inc(sem.ltg, 16)
     Y.dma_start(T.tabs[:], T.tab[:, :]).then_inc(sem.ltab, 16)
@@ -179,13 +172,13 @@ def rank_program(g, core, T, topo):
     g.wait_ge(sem.keyd, 2)
     lo = 2 * POS[rank]
     for dsts in KEY_CALLS[rank]:
-        spread([R[d] for d in dsts], T.kl[:, lo:lo + 2], T.key[:, 0:2], sem["kin%d" % rank])
+        send([(R[d], T.kl[:, lo:lo + 2], T.key[:, 0:2], sem["kin%d" % rank]) for d in dsts])
     if rank in KEY_RELAY:
         srcs, dsts = KEY_RELAY[rank]
         for s in srcs:
-            g.wait_ge(sem["kin%d" % s], 8)
+            g.wait_ge(sem["kin%d" % s], keys_in(s, rank))
         lo, hi = 2 * POS[srcs[0]], 2 * POS[srcs[-1]] + 2
-        spread([R[d] for d in dsts], T.kl[:, lo:hi], T.kl[:, lo:hi], sem["kin%d" % srcs[0]])
+        send([(R[d], T.kl[:, lo:hi], T.kl[:, lo:hi], sem["kin%d" % srcs[0]]) for d in dsts])
 
     def make_o(q):
         for n, j in enumerate(groups[q]):
@@ -197,7 +190,7 @@ def rank_program(g, core, T, topo):
                 src, c0 = T.key, 0
             else:
                 s = 2 if (rank == 0 and j == 4) else j
-                V.wait_ge(sem["kin%d" % s], 8)
+                V.wait_ge(sem["kin%d" % s], keys_in(s, rank))
                 src, c0 = T.kl, 2 * POS[j]
             for k in range(2):
                 V.tensor_scalar(T.sp[:, 64 * i + 32 * k:64 * i + 32 * k + 32], T.ones[:], src[:, c0 + k:c0 + k + 1], None,
@@ -228,17 +221,23 @@ def rank_program(g, core, T, topo):
             E.matmul_mx(T.z[:, c:c + b - a], T.tq[:, 128 * f:128 * f + 128], T.tqs[:, 128 * f:128 * f + 128],
                         T.oc[:, a:b], T.osc[:, a:b], True, True).then_inc(sem["z%d%d" % (f, q)], 1)
 
-    def make_e(q):
+    def copy(q, by_vector):
         a, b = 128 * first[q], 128 * first[q + 1]
         for f in range(4):
+            if (q in VCOPY[rank] and f % 2 == 0) != by_vector:
+                continue
             c = 512 * (f + 4 * (q % 2))
             out, src = T.et[:, 4 * a + f:4 * b:4], T.z[:, c:c + b - a]
-            if f % 2 == 0:
+            if by_vector:
                 V.wait_ge(sem["z%d%d" % (f, q)], 1)
                 V.tensor_copy(out, src).then_inc(sem["c%d" % q], 1)
             else:
                 S.wait_ge(sem["z%d%d" % (f, q)], 1)
                 S.activation(out, src, COPY).then_inc(sem["c%d" % q], 1)
+
+    def make_e(q):
+        copy(q, True)
+        a, b = 128 * first[q], 128 * first[q + 1]
         V.wait_ge(sem["c%d" % q], 4)
         V.quantize_mx(T.xc[:, a:b], T.xsc[:, a:b], T.et[:, 4 * a:4 * b]).then_inc(sem["e%d" % q], 1)
 
@@ -249,41 +248,41 @@ def rank_program(g, core, T, topo):
                       T.tabs[:, 512 * f:512 * f + 512]).then_inc(sem.tqd, 1)
     V.wait_ge(sem.lw, 16)
     V.quantize_mx(T.wq[:], T.wqs[:], T.ws[:]).then_inc(sem.wqd, 1)
-    make_z(0)
-    make_e(0)
-    for q in (1, 2, 3):
-        make_o(q)
+    for step in VSEQ[rank]:
+        (make_o if step[0] == "o" else make_e)(int(step[1]))
+    for q in range(len(groups)):
         make_z(q)
-        make_e(q)
+        copy(q, False)
 
-    for q in (1, 2, 3):
-        g.wait_ge(sem["e%d" % q], 1)
-        i0, dst = first[q], groups[q]
-        if (rank, dst[0]) in DIAG:
-            cs, ss = sem["cin%d" % rank], sem["sin%d" % rank]
-            send([(H["c%d%d" % (rank, j)], codes(T.ec, POS[rank]), codes(T.xc, i0 + n), cs) for n, j in enumerate(dst)])
-            if rank == 0:
-                send([(H["s0"], planes(T.esc, 0, 2), planes(T.xsc, i0, 2), ss)])
-            else:
-                hs = H["s24"] if rank in (2, 4) else H["s%d" % rank]
-                send([(hs, planes(T.esc, POS[rank]), planes(T.xsc, i0), ss)])
+    for step in SEND[rank]:
+        dst = [int(d) for d in step[1:]]
+        for q in range(1, len(groups)):
+            if [j for j in dst if j in groups[q]]:
+                g.wait_ge(sem["e%d" % q], 1)
+        diag = (rank, dst[0]) in DIAG
+        if step[0] == "C":
+            send([(H["c%d%d" % (rank, j)] if diag else R[j], codes(T.ec, POS[rank]), codes(T.xc, slot[j]),
+                   sem["cin%d" % rank]) for j in dst])
+        elif not diag:
+            send([(R[j], planes(T.esc, POS[rank]), planes(T.xsc, slot[j]), sem["sin%d" % rank]) for j in dst])
         else:
-            send([(R[j], codes(T.ec, POS[rank]), codes(T.xc, i0 + n), sem["cin%d" % rank]) for n, j in enumerate(dst)])
-            send([(R[j], planes(T.esc, POS[rank]), planes(T.xsc, i0 + n), sem["sin%d" % rank]) for n, j in enumerate(dst)])
+            to = {0: "s0", 1: "s1", 2: "s24", 3: "s3", 4: "s24"}[rank]
+            send([(H[to], planes(T.esc, POS[rank], len(dst)), planes(T.xsc, slot[dst[0]], len(dst)), sem["sin%d" % rank])])
 
     E.wait_ge(sem.wqd, 1)
     E.wait_ge(sem.e0, 1)
-    E.wait_ge(sem.c2, 4)
+    for q in range(len(groups)):
+        if q % 2 == 0 and q + 2 >= len(groups):
+            E.wait_ge(sem["c%d" % q], 4)
     far = [r for r in range(N) if (r, rank) in DIAG]
     near = [r for r in range(N) if r != rank and r not in far]
     E.matmul_mx(T.z[:, 0:128], T.wq[:], T.wqs[:], T.xc[:, 0:128], T.xsc[:, 0:128], True, False)
     todo = near + far
     for r in todo:
         p = 128 * POS[r]
-        direct = r in near
-        E.wait_ge(sem["cin%d" % r], fan(r, rank) if direct else 8)
-        if direct:
-            E.wait_ge(sem["sin%d" % r], fan(r, rank))
+        E.wait_ge(sem["cin%d" % r], fan(r, rank, "C") if r in near else 8)
+        if r in near:
+            E.wait_ge(sem["sin%d" % r], fan(r, rank, "S"))
         elif r == 0:
             E.wait_ge(sem.sin0, 4)
         else:

@@ -4,62 +4,73 @@ from concourse.mybir import dt, AluOpType, ActivationFunctionType
 
 N = 5
 POS = {0: 0, 1: 1, 3: 2, 2: 3, 4: 4}
-GROUPS = {0: [[0], [1], [2], [4], [3]],
-          1: [[1], [0], [2], [3], [4]],
-          2: [[2], [3], [0], [4, 1]],
-          3: [[3], [2], [4], [1], [0]],
-          4: [[4], [1], [0], [2, 3]]}
-VSEQ = {0: ["e0", "o1", "e1", "o2", "o3", "e2", "e3", "o4", "e4"],
-        1: ["e0", "o1", "o2", "e1", "e2", "o3", "e3", "o4", "e4"],
-        2: ["e0", "o1", "e1", "o2", "e2", "o3", "e3"],
-        3: ["e0", "o1", "o2", "e1", "e2", "o3", "e3", "o4", "e4"],
-        4: ["e0", "o1", "e1", "o2", "e2", "o3", "e3"]}
-VCOPY = {r: [0, 1, 2, 3, 4] for r in range(N)}
-SEND = {0: ["C1", "S1", "C2", "S24", "C4", "C3", "S3"],
-        1: ["C0", "S0", "C2", "S2", "C3", "S3", "C4", "S4"],
-        2: ["C3", "S3", "C0", "S0", "C41", "S41"],
-        3: ["C2", "S2", "C4", "S4", "C1", "S1", "C0", "S0"],
-        4: ["C1", "S1", "C0", "S0", "C23", "S23"]}
-KEY_CALLS = {0: [[1], [3]], 1: [[4], [0], [2]], 2: [[3], [4, 1]], 3: [[2], [0], [4]], 4: [[3], [2, 1]]}
+CFG = {
+    "ORDER": {0: [0, 2, 4, 1, 3], 1: [1, 0, 4, 3, 2], 2: [2, 0, 3, 4, 1], 3: [3, 2, 4, 1, 0], 4: [4, 1, 2, 0, 3]},
+    "VSEQ": {0: ["e0", "o1", "o2", "e1", "o3", "e2", "o4", "e3", "e4"],
+             1: ["o1", "e0", "o2", "e1", "o3", "e2", "e3", "o4", "e4"],
+             2: ["e0", "o2", "o1", "e1", "o3", "e2", "o4", "e3", "e4"],
+             3: ["e0", "o1", "o2", "e1", "o3", "e2", "e3", "o4", "e4"],
+             4: ["e0", "o1", "o2", "o3", "e1", "e2", "o4", "e3", "e4"]},
+    "SSEQ": {0: ["c0", "x1", "x2", "c1", "x3", "c2", "x4", "c3", "c4"],
+             1: ["x1", "c0", "x2", "x3", "c1", "c2", "x4", "c3", "c4"],
+             2: ["c0", "x2", "x1", "c1", "x3", "x4", "c2", "c3", "c4"],
+             3: ["c0", "x1", "x2", "c1", "x4", "x3", "c2", "c3", "c4"],
+             4: ["c0", "x1", "c1", "x2", "x3", "c2", "x4", "c3", "c4"]},
+    "VCOPY": {0: [[3], [0, 2, 3], [0, 2], [0], [1, 3]], 1: [[0, 2], [0, 2], [0, 2], [0], [1]],
+              2: [[1], [2], [0, 1], [0, 2, 3], [0, 2]], 3: [[0, 2, 3], [1], [0, 2], [0, 2], [0, 1]],
+              4: [[0, 2], [], [0, 2], [0, 2, 3], [1]]},
+    "SEND": {0: ["C2", "S2", "C4", "S4", "C3", "S1", "S3", "C1"], 1: ["S0", "C4", "S4", "C30", "S3", "C2", "S2"],
+             2: ["C0", "S03", "C3", "C4", "C1", "S14"], 3: ["C2", "C14", "S1", "S42", "C0", "S0"],
+             4: ["C1", "C2", "S2", "S0", "C0", "S1", "C3", "S3"]},
+    "HELP": {(0, 0, 0): ["K10", "C13"], (1, 1, 1): ["K21", "S02", "C20"], (1, 0, 1): ["K12", "C02", "S20", "C40"],
+             (2, 0, 0): ["K34", "C31"], (3, 1, 2): ["K30", "C04"], (3, 0, 1): ["S40"], (3, 0, 2): ["K42", "C34"],
+             (0, 0, 3): ["S31", "S13"], (1, 0, 0): ["S04"]},
+    "KEY_CALLS": {0: [[1], [3]], 1: [[4], [0], [2]], 2: [[3], [1], [4]], 3: [[2], [4], [0]], 4: [[3], [1], [2]]},
+}
 KEY_RELAY = {1: ([0], [2, 4]), 3: ([2, 4], [0]), 4: ([1], [3]), 2: ([3], [1])}
+NARROW = {(0, 3), (1, 0), (1, 2), (2, 1), (2, 4), (3, 0), (3, 4), (4, 1), (4, 2)}
 DIAG = {(0, 2), (0, 4), (2, 0), (4, 0), (1, 3), (3, 1)}
 BF, F32, MX, U8 = "bfloat16", "float32", "float8_e4m3fn_x4", "uint8"
 SCRATCH = {n: ("sbuf", [128, w], d) for n, w, d in (
-    ("tgs", 384, BF), ("tgt", 384, BF), ("tabs", 2048, BF), ("ws", 512, BF), ("kp", 1, F32), ("ex", 4, F32), ("e4", 4, BF),
-    ("kc", 4, F32), ("ones", 32, BF), ("g1", 4, BF), ("g2", 4, BF), ("p1", 4, F32), ("m1", 4, F32), ("key", 2, BF),
-    ("kl", 2 * N, BF), ("sp", 64 * N, BF), ("rows", 128 * N, BF), ("ot", 512 * N, BF), ("et", 512 * N, BF),
+    ("tgs", 384, BF), ("tgt", 384, BF), ("tabs", 2048, BF), ("ws", 512, BF), ("kp", 1, F32), ("ex", 1, F32), ("e4", 1, BF),
+    ("kc", 4, BF), ("zero", 32, BF), ("g1", 4, BF), ("g2", 4, BF), ("p1", 4, F32), ("m1", 4, F32), ("key", 4, BF),
+    ("key2", 2, BF), ("kl", 4 * N, BF), ("sp", 128 * N, BF), ("rows", 128 * N, BF), ("ot", 512 * N, BF), ("et", 512 * N, BF),
     ("tq", 512, MX), ("tqs", 512, U8), ("wq", 128, MX), ("wqs", 128, U8), ("oc", 128 * N, MX), ("osc", 128 * N, U8),
     ("xc", 128 * N, MX), ("xsc", 128 * N, U8), ("ec", 128 * N, MX), ("esc", 128 * N, U8), ("ysb", 128, F32))}
 SCRATCH["z"] = ("psum", [128, 4096], F32)
-SEMAPHORES = (["ltg", "ltab", "lw", "iot", "e4d", "kcd", "one", "tt", "gg1", "gg2", "pp1", "mm1", "keyd", "tqd", "wqd",
-               "yd", "yc", "yst", "sent"]
-              + ["%s%d" % (n, q) for q in range(5) for n in ("x", "r", "o", "q", "z0", "z1", "z2", "z3", "c", "e")]
-              + ["%s%d" % (n, r) for r in range(N) for n in ("kin", "cin", "sin")])
+SEMAPHORES = (["ltg", "ltab", "lw", "exd", "iot", "e4d", "kcd", "zd", "tto", "ttb", "ttp", "gg1", "gg2", "pp1", "mm1", "keyd",
+               "k2d", "tqd", "wqd", "yd", "yc", "yst", "sent"]
+              + ["%s%d" % (n, q) for q in range(N) for n in ("x", "r", "o", "q", "z0", "z1", "z2", "z3", "c", "e")]
+              + ["%s%d" % (n, r) for r in range(N) for n in ("kin", "cin", "sin")]
+              + ["h" + j for q in CFG["HELP"].values() for j in q])
 
 
 def helpers(T, topo):
-    def around(rank):
+    jobs, place = {}, {}
+    for (rank, near, i), js in CFG["HELP"].items():
         me = T.cores[rank]
-        on = [c for c in range(512) if topo.host(c) == topo.host(me) and topo.chip(c) == topo.chip(me) and c not in T.cores]
-        return [c for c in on if topo.die(c) == topo.die(me)], [c for c in on if topo.die(c) != topo.die(me)]
-    n1, f1 = around(1)
-    n0, f0 = around(0)
-    return {"c02": n1[2], "c04": f1[0], "s0": f1[2], "c20": f1[1], "c40": f1[3], "s24": n1[1],
-            "c13": n0[2], "s1": f0[0], "c31": f0[2], "s3": f0[3]}
+        on = [c for c in range(512) if topo.host(c) == topo.host(me) and topo.chip(c) == topo.chip(me) and c not in T.cores
+              and (topo.die(c) == topo.die(me)) == bool(near)]
+        jobs[on[i]] = js
+        for s, j in enumerate(js):
+            place[j] = (on[i], s)
+    return jobs, place
 
 
 def rank_program(g, core, T, topo):
     rank = T.rank_of(core)
-    H = helpers(T, topo)
+    jobs, place = helpers(T, topo)
+    if rank is None and core not in jobs:
+        return
     R = T.cores
     sem = T.sem
     sent = [0]
 
-    def codes(t, i, n=1):
-        return t[:, 128 * i:128 * (i + n)].bitcast(dt.uint8)
+    def codes(t, i):
+        return t[:, 128 * i:128 * i + 128].bitcast(dt.uint8)
 
-    def planes(t, i, n=1):
-        return t[:, 128 * i:128 * (i + n)]
+    def planes(t, i):
+        return t[:, 128 * i:128 * i + 128]
 
     def bits(m):
         return [e for e in range(16) if m >> e & 1]
@@ -67,18 +78,18 @@ def rank_program(g, core, T, topo):
     def here(c, d):
         return (topo.host(d), topo.chip(d)) == (topo.host(c), topo.chip(c))
 
-    def masks(c, dsts):
+    def masks(c, dsts, low=False):
         leave = [topo.mask(c, d) for d in R if topo.may_write(c, d) and not here(c, d)][0]
-        on = [here(c, d) for d in dsts]
+        on = [here(c, d) and not low for d in dsts]
         lists = []
         for i, d in enumerate(dsts):
-            pool = bits(topo.mask(c, d) & ~leave) if on[i] else bits(topo.mask(c, d))
+            pool = bits(topo.mask(c, d) & (~leave if on[i] else leave))
             k, w = on[:i].count(on[i]), len(pool) // on.count(on[i])
             lists.append(pool[k * w:k * w + w])
         return lists
 
-    def send(moves):
-        es = masks(core, [m[0] for m in moves])
+    def send(moves, low=False):
+        es = masks(core, [m[0] for m in moves], low)
         if len(moves) == 1:
             d, out, src, s = moves[0]
             rid, pid = topo.addr(d, core)
@@ -92,125 +103,146 @@ def rank_program(g, core, T, topo):
             g.remote_dma_fused(tr, local_sem=sem.sent)
         sent[0] += sum(len(l) for l in es)
 
-    def count(r, j, calls):
-        for q in calls:
-            if j in q:
-                to = [H["c%d%d" % (r, d)] if (r, d) in DIAG else R[d] for d in q]
-                return len(masks(R[r], to)[q.index(j)])
+    def width(c, dsts, d, low=False):
+        return len(masks(c, dsts, low)[dsts.index(d)])
 
-    def fan(r, j, kind):
-        return count(r, j, [[int(d) for d in s[1:]] for s in SEND[r] if s[0] == kind])
+    def e_to(kind, r, j):
+        name = "%s%d%d" % (kind, r, j)
+        if name in place:
+            return place[name] + (sem["h" + name],)
+        return R[j], POS[r], sem["%s%d" % ({"C": "cin", "S": "sin"}[kind], r)]
 
-    def keys_in(s, j):
+    def key_to(s, j):
+        name = "K%d%d" % (s, j)
+        return (place[name][0], sem["h" + name]) if name in place else (R[j], sem["kin%d" % s])
+
+    def e_in(kind, r, j, first_hop=False):
+        to = e_to(kind, r, j)[0]
+        if to != R[j] and not first_hop:
+            return width(to, [R[j]], R[j], True)
+        q = [[int(x) for x in s[1:]] for s in CFG["SEND"][r] if s[0] == kind and str(j) in s[1:]][0]
+        return width(R[r], [e_to(kind, r, x)[0] for x in q], to)
+
+    def keys_in(s, j, first_hop=False):
         if (s, j) in DIAG:
             via = [v for v in KEY_RELAY if s in KEY_RELAY[v][0] and j in KEY_RELAY[v][1]][0]
-            return count(via, j, [KEY_RELAY[via][1]])
-        return count(s, j, KEY_CALLS[s])
+            return width(R[via], [R[d] for d in KEY_RELAY[via][1]], R[j], True)
+        to = key_to(s, j)[0]
+        if to != R[j] and not first_hop:
+            return width(to, [R[j]], R[j], True)
+        q = [q for q in CFG["KEY_CALLS"][s] if j in q][0]
+        return width(R[s], [key_to(s, d)[0] for d in q], to, True)
 
     if rank is None:
-        names = [n for n in H if H[n] == core]
-        if not names:
-            return
-        name = names[0]
-        if name[0] == "c":
-            r, j = int(name[1]), int(name[2])
-            g.wait_ge(sem["cin%d" % r], fan(r, j, "C"))
-            send([(R[j], codes(T.ec, POS[r]), codes(T.ec, POS[r]), sem["cin%d" % r])])
-        elif name == "s0":
-            g.wait_ge(sem.sin0, 8)
-            send([(R[2], planes(T.esc, POS[0]), planes(T.esc, 0), sem.sin0),
-                  (R[4], planes(T.esc, POS[0]), planes(T.esc, 1), sem.sin0)])
-        elif name == "s24":
-            g.wait_ge(sem.sin2, 8)
-            g.wait_ge(sem.sin4, 8)
-            send([(R[0], planes(T.esc, POS[2], 2), planes(T.esc, POS[2], 2), sem.sin2)])
-        else:
-            r = int(name[1])
-            g.wait_ge(sem["sin%d" % r], 8)
-            send([(R[4 - r], planes(T.esc, POS[r]), planes(T.esc, POS[r]), sem["sin%d" % r])])
+        for s, job in enumerate(jobs[core]):
+            kind, r, j = job[0], int(job[1]), int(job[2])
+            g.wait_ge(sem["h" + job], keys_in(r, j, True) if kind == "K" else e_in(kind, r, j, True))
+            if kind == "K":
+                lo = 4 * POS[r]
+                send([(R[j], T.kl[:, lo:lo + 2], T.kl[:, lo:lo + 2], sem["kin%d" % r])], True)
+            elif kind == "C":
+                send([(R[j], codes(T.ec, POS[r]), codes(T.ec, s), sem["cin%d" % r])], True)
+            else:
+                send([(R[j], planes(T.esc, POS[r]), planes(T.esc, s), sem["sin%d" % r])], True)
         g.wait_ge(sem.sent, sent[0])
         return
 
     V, S, E, Y = g.vector, g.scalar, g.tensor, g.sync
     EQ, MUL, ADD = AluOpType.is_equal, AluOpType.mult, AluOpType.add
-    EXP, COPY = ActivationFunctionType.Exp, ActivationFunctionType.Copy
+    EXP, COPY, IDENT = ActivationFunctionType.Exp, ActivationFunctionType.Copy, ActivationFunctionType.Identity
     LN2 = math.log(2.0)
-    groups = GROUPS[rank]
-    first = [0]
-    for q in groups:
-        first.append(first[-1] + len(q))
-    slot = {j: i for i, j in enumerate([j for q in groups for j in q])}
+    order = CFG["ORDER"][rank]
+    narrow_in = [s for s, j in NARROW if j == rank]
+    narrow_out = [j for s, j in NARROW if s == rank]
 
     Y.dma_start(T.tgs[:], T.tg[:, :]).then_inc(sem.ltg, 16)
     Y.dma_start(T.tabs[:], T.tab[:, :]).then_inc(sem.ltab, 16)
     Y.dma_start(T.ws[:], T.w[:, :]).then_inc(sem.lw, 16)
 
-    g.iota(T.ex[:], [[1, 4]], 4 * rank, 0, allow_small_or_imprecise_dtypes=True).then_inc(sem.iot, 1)
-    g.iota(T.kp[:], [[1, 1]], 128, 1, allow_small_or_imprecise_dtypes=True).then_inc(sem.iot, 1)
-    S.wait_ge(sem.iot, 2)
+    V.memset(T.ex[:], 4.0 * rank).then_inc(sem.exd, 1)
+    S.wait_ge(sem.exd, 1)
     S.activation(T.e4[:], T.ex[:], EXP, scale=LN2).then_inc(sem.e4d, 1)
-    V.memset(T.ones[:], 1.0).then_inc(sem.one, 1)
-    V.wait_ge(sem.iot, 2)
-    V.wait_ge(sem.e4d, 1)
-    V.tensor_scalar(T.kc[:], T.e4[:], T.kp[:, 0:1], None, MUL).then_inc(sem.kcd, 1)
+    g.iota(T.kp[:], [[1, 1]], 128, 1, allow_small_or_imprecise_dtypes=True).then_inc(sem.iot, 1)
+    V.memset(T.zero[:], 0.0).then_inc(sem.zd, 1)
 
     V.wait_ge(sem.ltg, 16)
-    V.transpose(T.tgt[:], T.tgs[:]).then_inc(sem.tt, 1)
-    S.wait_ge(sem.tt, 1)
+    for a, s in ((0, sem.tto), (256, sem.ttb), (128, sem.ttp)):
+        V.transpose(T.tgt[:, a:a + 128], T.tgs[:, a:a + 128]).then_inc(s, 1)
+    S.wait_ge(sem.tto, 1)
     S.activation(T.g1[:], T.tgt[:, 0:128:32], EXP, scale=4 * LN2).then_inc(sem.gg1, 1)
+    S.wait_ge(sem.ttb, 1)
     S.activation(T.g2[:], T.tgt[:, 256:384:32], EXP, scale=LN2).then_inc(sem.gg2, 1)
-    V.wait_ge(sem.tt, 1)
+    V.wait_ge(sem.ttp, 1)
     V.tensor_scalar(T.p1[:], T.tgt[:, 128:256:32], 128.0, None, ADD).then_inc(sem.pp1, 1)
     V.wait_ge(sem.pp1, 1)
     V.wait_ge(sem.gg1, 1)
     V.tensor_tensor(T.m1[:], T.p1[:], T.g1[:], MUL).then_inc(sem.mm1, 1)
     V.wait_ge(sem.mm1, 1)
     V.wait_ge(sem.gg2, 1)
-    V.tensor_tensor(T.key[0:64, 0:2], T.m1[0:64, 0:2], T.g2[0:64, 0:2], MUL).then_inc(sem.keyd, 1)
-    V.tensor_tensor(T.key[64:128, 0:2], T.m1[64:128, 2:4], T.g2[64:128, 2:4], MUL).then_inc(sem.keyd, 1)
+    V.tensor_tensor(T.key[:], T.m1[:], T.g2[:], MUL).then_inc(sem.keyd, 1)
+    if narrow_out:
+        V.wait_ge(sem.keyd, 1)
+        V.tensor_copy(T.key2[0:64, 0:2], T.key[0:64, 0:2]).then_inc(sem.k2d, 1)
+        V.tensor_copy(T.key2[64:128, 0:2], T.key[64:128, 2:4]).then_inc(sem.k2d, 1)
+    V.wait_ge(sem.iot, 1)
+    V.wait_ge(sem.e4d, 1)
+    for f in range(4):
+        V.tensor_scalar(T.kc[:, f:f + 1], T.kp[:], T.e4[:, 0:1], 2.0 ** f, MUL, MUL).then_inc(sem.kcd, 1)
 
-    g.wait_ge(sem.keyd, 2)
-    lo = 2 * POS[rank]
-    for dsts in KEY_CALLS[rank]:
-        send([(R[d], T.kl[:, lo:lo + 2], T.key[:, 0:2], sem["kin%d" % rank]) for d in dsts])
+    g.wait_ge(sem.keyd, 1)
+    lo = 4 * POS[rank]
+    for dsts in CFG["KEY_CALLS"][rank]:
+        if dsts[0] in narrow_out:
+            g.wait_ge(sem.k2d, 2)
+        w, src = (2, T.key2) if dsts[0] in narrow_out else (4, T.key)
+        send([(key_to(rank, d)[0], T.kl[:, lo:lo + w], src[:], key_to(rank, d)[1]) for d in dsts], True)
     if rank in KEY_RELAY:
         srcs, dsts = KEY_RELAY[rank]
         for s in srcs:
             g.wait_ge(sem["kin%d" % s], keys_in(s, rank))
-        lo, hi = 2 * POS[srcs[0]], 2 * POS[srcs[-1]] + 2
-        send([(R[d], T.kl[:, lo:hi], T.kl[:, lo:hi], sem["kin%d" % srcs[0]]) for d in dsts])
+        lo, hi = 4 * POS[srcs[0]], 4 * POS[srcs[-1]] + 4
+        send([(R[d], T.kl[:, lo:hi], T.kl[:, lo:hi], sem["kin%d" % srcs[0]]) for d in dsts], True)
+
+    def spread(q, by_vector):
+        W, j = (V if by_vector else S), order[q]
+        W.wait_ge(sem.zd, 1)
+        if j == rank:
+            W.wait_ge(sem.keyd, 1)
+            src, c0 = T.key, 0
+        else:
+            s = 2 if (rank == 0 and j == 4) else j
+            W.wait_ge(sem["kin%d" % s], keys_in(s, rank))
+            src, c0 = T.kl, 4 * POS[j]
+        for k in range(2 if j in narrow_in else 4):
+            out, one = T.sp[:, 128 * q + 32 * k:128 * q + 32 * k + 32], src[:, c0 + k:c0 + k + 1]
+            if k % 2 == 0 and by_vector:
+                V.tensor_scalar(out, T.zero[:], one, None, ADD).then_inc(sem["x%d" % q], 1)
+            elif k % 2 and not by_vector:
+                S.activation(out, T.zero[:], IDENT, bias=one).then_inc(sem["x%d" % q], 1)
 
     def make_o(q):
-        for n, j in enumerate(groups[q]):
-            i = first[q] + n
-            if j == rank:
-                V.wait_ge(sem.keyd, 2)
-                V.wait_ge(sem.one, 1)
-                V.wait_ge(sem.kcd, 1)
-                src, c0 = T.key, 0
-            else:
-                s = 2 if (rank == 0 and j == 4) else j
-                V.wait_ge(sem["kin%d" % s], keys_in(s, rank))
-                src, c0 = T.kl, 2 * POS[j]
-            for k in range(2):
-                V.tensor_scalar(T.sp[:, 64 * i + 32 * k:64 * i + 32 * k + 32], T.ones[:], src[:, c0 + k:c0 + k + 1], None,
-                                MUL).then_inc(sem["x%d" % q], 1)
-        V.wait_ge(sem["x%d" % q], 2 * len(groups[q]))
-        for n in range(len(groups[q])):
-            i = first[q] + n
+        a, b = 128 * q, 128 * q + 128
+        spread(q, True)
+        if order[q] in narrow_in:
+            V.wait_ge(sem["x%d" % q], 2)
             for h in range(2):
                 for to in range(2):
-                    V.transpose(T.rows[64 * to:64 * to + 64, 128 * i + 64 * h:128 * i + 64 * h + 64],
-                                T.sp[64 * h:64 * h + 64, 64 * i:64 * i + 64]).then_inc(sem["r%d" % q], 1)
-        V.wait_ge(sem["r%d" % q], 4 * len(groups[q]))
-        a, b = 128 * first[q], 128 * first[q + 1]
+                    V.transpose(T.rows[64 * to:64 * to + 64, a + 64 * h:a + 64 * h + 64],
+                                T.sp[64 * h:64 * h + 64, a:a + 64]).then_inc(sem["r%d" % q], 1)
+            V.wait_ge(sem["r%d" % q], 4)
+        else:
+            V.wait_ge(sem["x%d" % q], 4)
+            V.transpose(T.rows[:, a:b], T.sp[:, a:b]).then_inc(sem["r%d" % q], 1)
+            V.wait_ge(sem["r%d" % q], 1)
+        if q == 0:
+            V.wait_ge(sem.kcd, 4)
         for f in range(4):
             V.tensor_scalar(T.ot[:, 4 * a + f:4 * b:4], T.rows[:, a:b], T.kc[:, f:f + 1], None, EQ).then_inc(sem["o%d" % q], 1)
         V.wait_ge(sem["o%d" % q], 4)
         V.quantize_mx(T.oc[:, a:b], T.osc[:, a:b], T.ot[:, 4 * a:4 * b]).then_inc(sem["q%d" % q], 1)
 
     def make_z(q):
-        a, b = 128 * first[q], 128 * first[q + 1]
+        a, b = 128 * q, 128 * q + 128
         E.wait_ge(sem["q%d" % q], 1)
         if q == 0:
             E.wait_ge(sem.tqd, 4)
@@ -218,16 +250,16 @@ def rank_program(g, core, T, topo):
             E.wait_ge(sem["c%d" % (q - 2)], 4)
         for f in range(4):
             c = 512 * (f + 4 * (q % 2))
-            E.matmul_mx(T.z[:, c:c + b - a], T.tq[:, 128 * f:128 * f + 128], T.tqs[:, 128 * f:128 * f + 128],
+            E.matmul_mx(T.z[:, c:c + 128], T.tq[:, 128 * f:128 * f + 128], T.tqs[:, 128 * f:128 * f + 128],
                         T.oc[:, a:b], T.osc[:, a:b], True, True).then_inc(sem["z%d%d" % (f, q)], 1)
 
     def copy(q, by_vector):
-        a, b = 128 * first[q], 128 * first[q + 1]
+        a, b = 128 * q, 128 * q + 128
         for f in range(4):
-            if (q in VCOPY[rank] and f % 2 == 0) != by_vector:
+            if (f in CFG["VCOPY"][rank][q]) != by_vector:
                 continue
             c = 512 * (f + 4 * (q % 2))
-            out, src = T.et[:, 4 * a + f:4 * b:4], T.z[:, c:c + b - a]
+            out, src = T.et[:, 4 * a + f:4 * b:4], T.z[:, c:c + 128]
             if by_vector:
                 V.wait_ge(sem["z%d%d" % (f, q)], 1)
                 V.tensor_copy(out, src).then_inc(sem["c%d" % q], 1)
@@ -237,7 +269,7 @@ def rank_program(g, core, T, topo):
 
     def make_e(q):
         copy(q, True)
-        a, b = 128 * first[q], 128 * first[q + 1]
+        a, b = 128 * q, 128 * q + 128
         V.wait_ge(sem["c%d" % q], 4)
         V.quantize_mx(T.xc[:, a:b], T.xsc[:, a:b], T.et[:, 4 * a:4 * b]).then_inc(sem["e%d" % q], 1)
 
@@ -248,45 +280,40 @@ def rank_program(g, core, T, topo):
                       T.tabs[:, 512 * f:512 * f + 512]).then_inc(sem.tqd, 1)
     V.wait_ge(sem.lw, 16)
     V.quantize_mx(T.wq[:], T.wqs[:], T.ws[:]).then_inc(sem.wqd, 1)
-    for step in VSEQ[rank]:
+    for step in CFG["VSEQ"][rank]:
         (make_o if step[0] == "o" else make_e)(int(step[1]))
-    for q in range(len(groups)):
-        make_z(q)
-        copy(q, False)
-
-    for step in SEND[rank]:
-        dst = [int(d) for d in step[1:]]
-        for q in range(1, len(groups)):
-            if [j for j in dst if j in groups[q]]:
-                g.wait_ge(sem["e%d" % q], 1)
-        diag = (rank, dst[0]) in DIAG
-        if step[0] == "C":
-            send([(H["c%d%d" % (rank, j)] if diag else R[j], codes(T.ec, POS[rank]), codes(T.xc, slot[j]),
-                   sem["cin%d" % rank]) for j in dst])
-        elif not diag:
-            send([(R[j], planes(T.esc, POS[rank]), planes(T.xsc, slot[j]), sem["sin%d" % rank]) for j in dst])
+    spread(0, False)
+    for step in CFG["SSEQ"][rank]:
+        if step[0] == "x":
+            spread(int(step[1]), False)
         else:
-            to = {0: "s0", 1: "s1", 2: "s24", 3: "s3", 4: "s24"}[rank]
-            send([(H[to], planes(T.esc, POS[rank], len(dst)), planes(T.xsc, slot[dst[0]], len(dst)), sem["sin%d" % rank])])
+            copy(int(step[1]), False)
+    for q in range(N):
+        make_z(q)
+
+    for step in CFG["SEND"][rank]:
+        kind, dst = step[0], [int(d) for d in step[1:]]
+        for j in dst:
+            g.wait_ge(sem["e%d" % order.index(j)], 1)
+        moves = []
+        for j in dst:
+            c, s, up = e_to(kind, rank, j)
+            q = order.index(j)
+            moves.append((c, codes(T.ec, s), codes(T.xc, q), up) if kind == "C" else
+                         (c, planes(T.esc, s), planes(T.xsc, q), up))
+        send(moves)
 
     E.wait_ge(sem.wqd, 1)
     E.wait_ge(sem.e0, 1)
-    for q in range(len(groups)):
-        if q % 2 == 0 and q + 2 >= len(groups):
-            E.wait_ge(sem["c%d" % q], 4)
+    E.wait_ge(sem.c4, 4)
     far = [r for r in range(N) if (r, rank) in DIAG]
     near = [r for r in range(N) if r != rank and r not in far]
     E.matmul_mx(T.z[:, 0:128], T.wq[:], T.wqs[:], T.xc[:, 0:128], T.xsc[:, 0:128], True, False)
     todo = near + far
     for r in todo:
         p = 128 * POS[r]
-        E.wait_ge(sem["cin%d" % r], fan(r, rank, "C") if r in near else 8)
-        if r in near:
-            E.wait_ge(sem["sin%d" % r], fan(r, rank, "S"))
-        elif r == 0:
-            E.wait_ge(sem.sin0, 4)
-        else:
-            E.wait_ge(sem["sin%d" % (2 if rank == 0 else r)], 8)
+        E.wait_ge(sem["cin%d" % r], e_in("C", r, rank))
+        E.wait_ge(sem["sin%d" % r], e_in("S", r, rank))
         last = r == todo[-1]
         m = E.matmul_mx(T.z[:, 0:128], T.wq[:], T.wqs[:], T.ec[:, p:p + 128], T.esc[:, p:p + 128], False, last)
         if last:

import math
from concourse.bass import DstId, RemoteDMATransfer
from concourse.mybir import dt, AluOpType, ActivationFunctionType

N = 5
POS = {0: 0, 1: 1, 3: 2, 2: 3, 4: 4}
CFG = {
    "ORDER": {0: [0, 2, 4, 1, 3], 1: [1, 0, 4, 3, 2], 2: [2, 0, 3, 4, 1], 3: [3, 2, 4, 1, 0], 4: [4, 1, 2, 0, 3]},
    "VSEQ": {0: ["e0", "o1", "o2", "e1", "o3", "e2", "o4", "e3", "e4"],
             1: ["o1", "e0", "o2", "e1", "o3", "e2", "e3", "o4", "e4"],
             2: ["e0", "o2", "o1", "e1", "o3", "e2", "o4", "e3", "e4"],
             3: ["e0", "o1", "o2", "e1", "o3", "e2", "e3", "o4", "e4"],
             4: ["e0", "o1", "o2", "o3", "e1", "e2", "o4", "e3", "e4"]},
    "SSEQ": {0: ["c0", "x1", "x2", "c1", "x3", "c2", "x4", "c3", "c4"],
             1: ["x1", "c0", "x2", "x3", "c1", "c2", "x4", "c3", "c4"],
             2: ["c0", "x2", "x1", "c1", "x3", "x4", "c2", "c3", "c4"],
             3: ["c0", "x1", "x2", "c1", "x4", "x3", "c2", "c3", "c4"],
             4: ["c0", "x1", "c1", "x2", "x3", "c2", "x4", "c3", "c4"]},
    "VCOPY": {0: [[3], [0, 2, 3], [0, 2], [0], [1, 3]], 1: [[0, 2], [0, 2], [0, 2], [0], [1]],
              2: [[1], [2], [0, 1], [0, 2, 3], [0, 2]], 3: [[0, 2, 3], [1], [0, 2], [0, 2], [0, 1]],
              4: [[0, 2], [], [0, 2], [0, 2, 3], [1]]},
    "SEND": {0: ["C2", "S2", "C4", "S4", "C3", "S1", "S3", "C1"], 1: ["S0", "C4", "S4", "C30", "S3", "C2", "S2"],
             2: ["C0", "S03", "C3", "C4", "C1", "S14"], 3: ["C2", "C14", "S1", "S42", "C0", "S0"],
             4: ["C1", "C2", "S2", "S0", "C0", "S1", "C3", "S3"]},
    "HELP": {(0, 0, 0): ["K10", "C13"], (1, 1, 1): ["K21", "S02", "C20"], (1, 0, 1): ["K12", "C02", "S20", "C40"],
             (2, 0, 0): ["K34", "C31"], (3, 1, 2): ["K30", "C04"], (3, 0, 1): ["S40"], (3, 0, 2): ["K42", "C34"],
             (0, 0, 3): ["S31", "S13"], (1, 0, 0): ["S04"]},
    "KEY_CALLS": {0: [[1], [3]], 1: [[4], [0], [2]], 2: [[3], [1], [4]], 3: [[2], [4], [0]], 4: [[3], [1], [2]]},
}
KEY_RELAY = {1: ([0], [2, 4]), 3: ([2, 4], [0]), 4: ([1], [3]), 2: ([3], [1])}
NARROW = {(0, 3), (1, 0), (1, 2), (2, 1), (2, 4), (3, 0), (3, 4), (4, 1), (4, 2)}
DIAG = {(0, 2), (0, 4), (2, 0), (4, 0), (1, 3), (3, 1)}
BF, F32, MX, U8 = "bfloat16", "float32", "float8_e4m3fn_x4", "uint8"
SCRATCH = {n: ("sbuf", [128, w], d) for n, w, d in (
    ("tgs", 384, BF), ("tgt", 384, BF), ("tabs", 2048, BF), ("ws", 512, BF), ("kp", 1, F32), ("ex", 1, F32), ("e4", 1, BF),
    ("kc", 4, BF), ("zero", 32, BF), ("g1", 4, BF), ("g2", 4, BF), ("p1", 4, F32), ("m1", 4, F32), ("key", 4, BF),
    ("key2", 2, BF), ("kl", 4 * N, BF), ("sp", 128 * N, BF), ("rows", 128 * N, BF), ("ot", 512 * N, BF), ("et", 512 * N, BF),
    ("tq", 512, MX), ("tqs", 512, U8), ("wq", 128, MX), ("wqs", 128, U8), ("oc", 128 * N, MX), ("osc", 128 * N, U8),
    ("xc", 128 * N, MX), ("xsc", 128 * N, U8), ("ec", 128 * N, MX), ("esc", 128 * N, U8), ("ysb", 128, F32))}
SCRATCH["z"] = ("psum", [128, 4096], F32)
SEMAPHORES = (["ltg", "ltab", "lw", "exd", "iot", "e4d", "kcd", "zd", "tto", "ttb", "ttp", "gg1", "gg2", "pp1", "mm1", "keyd",
               "k2d", "tqd", "wqd", "yd", "yc", "yst", "sent"]
              + ["%s%d" % (n, q) for q in range(N) for n in ("x", "r", "o", "q", "z0", "z1", "z2", "z3", "c", "e")]
              + ["%s%d" % (n, r) for r in range(N) for n in ("kin", "cin", "sin")]
              + ["h" + j for q in CFG["HELP"].values() for j in q])


def helpers(T, topo):
    jobs, place = {}, {}
    for (rank, near, i), js in CFG["HELP"].items():
        me = T.cores[rank]
        on = [c for c in range(512) if topo.host(c) == topo.host(me) and topo.chip(c) == topo.chip(me) and c not in T.cores
              and (topo.die(c) == topo.die(me)) == bool(near)]
        jobs[on[i]] = js
        for s, j in enumerate(js):
            place[j] = (on[i], s)
    return jobs, place


def rank_program(g, core, T, topo):
    rank = T.rank_of(core)
    jobs, place = helpers(T, topo)
    if rank is None and core not in jobs:
        return
    R = T.cores
    sem = T.sem
    sent = [0]

    def codes(t, i):
        return t[:, 128 * i:128 * i + 128].bitcast(dt.uint8)

    def planes(t, i):
        return t[:, 128 * i:128 * i + 128]

    def bits(m):
        return [e for e in range(16) if m >> e & 1]

    def here(c, d):
        return (topo.host(d), topo.chip(d)) == (topo.host(c), topo.chip(c))

    def masks(c, dsts, low=False):
        leave = [topo.mask(c, d) for d in R if topo.may_write(c, d) and not here(c, d)][0]
        on = [here(c, d) and not low for d in dsts]
        lists = []
        for i, d in enumerate(dsts):
            pool = bits(topo.mask(c, d) & (~leave if on[i] else leave))
            k, w = on[:i].count(on[i]), len(pool) // on.count(on[i])
            lists.append(pool[k * w:k * w + w])
        return lists

    def send(moves, low=False):
        es = masks(core, [m[0] for m in moves], low)
        if len(moves) == 1:
            d, out, src, s = moves[0]
            rid, pid = topo.addr(d, core)
            g.remote_dma(out, src, s, sem.sent, pid, rid, sum(1 << e for e in es[0]))
        else:
            tr = []
            for (d, out, src, s), l in zip(moves, es):
                rid, pid = topo.addr(d, core)
                tr.append(RemoteDMATransfer(dst_ids=[DstId(rid=rid, pnc=pid)], dma_engine_mask=sum(1 << e for e in l),
                                            remote_sem=s, src=src, dst=out))
            g.remote_dma_fused(tr, local_sem=sem.sent)
        sent[0] += sum(len(l) for l in es)

    def width(c, dsts, d, low=False):
        return len(masks(c, dsts, low)[dsts.index(d)])

    def e_to(kind, r, j):
        name = "%s%d%d" % (kind, r, j)
        if name in place:
            return place[name] + (sem["h" + name],)
        return R[j], POS[r], sem["%s%d" % ({"C": "cin", "S": "sin"}[kind], r)]

    def key_to(s, j):
        name = "K%d%d" % (s, j)
        return (place[name][0], sem["h" + name]) if name in place else (R[j], sem["kin%d" % s])

    def e_in(kind, r, j, first_hop=False):
        to = e_to(kind, r, j)[0]
        if to != R[j] and not first_hop:
            return width(to, [R[j]], R[j], True)
        q = [[int(x) for x in s[1:]] for s in CFG["SEND"][r] if s[0] == kind and str(j) in s[1:]][0]
        return width(R[r], [e_to(kind, r, x)[0] for x in q], to)

    def keys_in(s, j, first_hop=False):
        if (s, j) in DIAG:
            via = [v for v in KEY_RELAY if s in KEY_RELAY[v][0] and j in KEY_RELAY[v][1]][0]
            return width(R[via], [R[d] for d in KEY_RELAY[via][1]], R[j], True)
        to = key_to(s, j)[0]
        if to != R[j] and not first_hop:
            return width(to, [R[j]], R[j], True)
        q = [q for q in CFG["KEY_CALLS"][s] if j in q][0]
        return width(R[s], [key_to(s, d)[0] for d in q], to, True)

    if rank is None:
        for s, job in enumerate(jobs[core]):
            kind, r, j = job[0], int(job[1]), int(job[2])
            g.wait_ge(sem["h" + job], keys_in(r, j, True) if kind == "K" else e_in(kind, r, j, True))
            if kind == "K":
                lo = 4 * POS[r]
                send([(R[j], T.kl[:, lo:lo + 2], T.kl[:, lo:lo + 2], sem["kin%d" % r])], True)
            elif kind == "C":
                send([(R[j], codes(T.ec, POS[r]), codes(T.ec, s), sem["cin%d" % r])], True)
            else:
                send([(R[j], planes(T.esc, POS[r]), planes(T.esc, s), sem["sin%d" % r])], True)
        g.wait_ge(sem.sent, sent[0])
        return

    V, S, E, Y = g.vector, g.scalar, g.tensor, g.sync
    EQ, MUL, ADD = AluOpType.is_equal, AluOpType.mult, AluOpType.add
    EXP, COPY, IDENT = ActivationFunctionType.Exp, ActivationFunctionType.Copy, ActivationFunctionType.Identity
    LN2 = math.log(2.0)
    order = CFG["ORDER"][rank]
    narrow_in = [s for s, j in NARROW if j == rank]
    narrow_out = [j for s, j in NARROW if s == rank]

    Y.dma_start(T.tgs[:], T.tg[:, :]).then_inc(sem.ltg, 16)
    Y.dma_start(T.tabs[:], T.tab[:, :]).then_inc(sem.ltab, 16)
    Y.dma_start(T.ws[:], T.w[:, :]).then_inc(sem.lw, 16)

    V.memset(T.ex[:], 4.0 * rank).then_inc(sem.exd, 1)
    S.wait_ge(sem.exd, 1)
    S.activation(T.e4[:], T.ex[:], EXP, scale=LN2).then_inc(sem.e4d, 1)
    g.iota(T.kp[:], [[1, 1]], 128, 1, allow_small_or_imprecise_dtypes=True).then_inc(sem.iot, 1)
    V.memset(T.zero[:], 0.0).then_inc(sem.zd, 1)

    V.wait_ge(sem.ltg, 16)
    for a, s in ((0, sem.tto), (256, sem.ttb), (128, sem.ttp)):
        V.transpose(T.tgt[:, a:a + 128], T.tgs[:, a:a + 128]).then_inc(s, 1)
    S.wait_ge(sem.tto, 1)
    S.activation(T.g1[:], T.tgt[:, 0:128:32], EXP, scale=4 * LN2).then_inc(sem.gg1, 1)
    S.wait_ge(sem.ttb, 1)
    S.activation(T.g2[:], T.tgt[:, 256:384:32], EXP, scale=LN2).then_inc(sem.gg2, 1)
    V.wait_ge(sem.ttp, 1)
    V.tensor_scalar(T.p1[:], T.tgt[:, 128:256:32], 128.0, None, ADD).then_inc(sem.pp1, 1)
    V.wait_ge(sem.pp1, 1)
    V.wait_ge(sem.gg1, 1)
    V.tensor_tensor(T.m1[:], T.p1[:], T.g1[:], MUL).then_inc(sem.mm1, 1)
    V.wait_ge(sem.mm1, 1)
    V.wait_ge(sem.gg2, 1)
    V.tensor_tensor(T.key[:], T.m1[:], T.g2[:], MUL).then_inc(sem.keyd, 1)
    if narrow_out:
        V.wait_ge(sem.keyd, 1)
        V.tensor_copy(T.key2[0:64, 0:2], T.key[0:64, 0:2]).then_inc(sem.k2d, 1)
        V.tensor_copy(T.key2[64:128, 0:2], T.key[64:128, 2:4]).then_inc(sem.k2d, 1)
    V.wait_ge(sem.iot, 1)
    V.wait_ge(sem.e4d, 1)
    for f in range(4):
        V.tensor_scalar(T.kc[:, f:f + 1], T.kp[:], T.e4[:, 0:1], 2.0 ** f, MUL, MUL).then_inc(sem.kcd, 1)

    g.wait_ge(sem.keyd, 1)
    lo = 4 * POS[rank]
    for dsts in CFG["KEY_CALLS"][rank]:
        if dsts[0] in narrow_out:
            g.wait_ge(sem.k2d, 2)
        w, src = (2, T.key2) if dsts[0] in narrow_out else (4, T.key)
        send([(key_to(rank, d)[0], T.kl[:, lo:lo + w], src[:], key_to(rank, d)[1]) for d in dsts], True)
    if rank in KEY_RELAY:
        srcs, dsts = KEY_RELAY[rank]
        for s in srcs:
            g.wait_ge(sem["kin%d" % s], keys_in(s, rank))
        lo, hi = 4 * POS[srcs[0]], 4 * POS[srcs[-1]] + 4
        send([(R[d], T.kl[:, lo:hi], T.kl[:, lo:hi], sem["kin%d" % srcs[0]]) for d in dsts], True)

    def spread(q, by_vector):
        W, j = (V if by_vector else S), order[q]
        W.wait_ge(sem.zd, 1)
        if j == rank:
            W.wait_ge(sem.keyd, 1)
            src, c0 = T.key, 0
        else:
            s = 2 if (rank == 0 and j == 4) else j
            W.wait_ge(sem["kin%d" % s], keys_in(s, rank))
            src, c0 = T.kl, 4 * POS[j]
        for k in range(2 if j in narrow_in else 4):
            out, one = T.sp[:, 128 * q + 32 * k:128 * q + 32 * k + 32], src[:, c0 + k:c0 + k + 1]
            if k % 2 == 0 and by_vector:
                V.tensor_scalar(out, T.zero[:], one, None, ADD).then_inc(sem["x%d" % q], 1)
            elif k % 2 and not by_vector:
                S.activation(out, T.zero[:], IDENT, bias=one).then_inc(sem["x%d" % q], 1)

    def make_o(q):
        a, b = 128 * q, 128 * q + 128
        spread(q, True)
        if order[q] in narrow_in:
            V.wait_ge(sem["x%d" % q], 2)
            for h in range(2):
                for to in range(2):
                    V.transpose(T.rows[64 * to:64 * to + 64, a + 64 * h:a + 64 * h + 64],
                                T.sp[64 * h:64 * h + 64, a:a + 64]).then_inc(sem["r%d" % q], 1)
            V.wait_ge(sem["r%d" % q], 4)
        else:
            V.wait_ge(sem["x%d" % q], 4)
            V.transpose(T.rows[:, a:b], T.sp[:, a:b]).then_inc(sem["r%d" % q], 1)
            V.wait_ge(sem["r%d" % q], 1)
        if q == 0:
            V.wait_ge(sem.kcd, 4)
        for f in range(4):
            V.tensor_scalar(T.ot[:, 4 * a + f:4 * b:4], T.rows[:, a:b], T.kc[:, f:f + 1], None, EQ).then_inc(sem["o%d" % q], 1)
        V.wait_ge(sem["o%d" % q], 4)
        V.quantize_mx(T.oc[:, a:b], T.osc[:, a:b], T.ot[:, 4 * a:4 * b]).then_inc(sem["q%d" % q], 1)

    def make_z(q):
        a, b = 128 * q, 128 * q + 128
        E.wait_ge(sem["q%d" % q], 1)
        if q == 0:
            E.wait_ge(sem.tqd, 4)
        if q >= 2:
            E.wait_ge(sem["c%d" % (q - 2)], 4)
        for f in range(4):
            c = 512 * (f + 4 * (q % 2))
            E.matmul_mx(T.z[:, c:c + 128], T.tq[:, 128 * f:128 * f + 128], T.tqs[:, 128 * f:128 * f + 128],
                        T.oc[:, a:b], T.osc[:, a:b], True, True).then_inc(sem["z%d%d" % (f, q)], 1)

    def copy(q, by_vector):
        a, b = 128 * q, 128 * q + 128
        for f in range(4):
            if (f in CFG["VCOPY"][rank][q]) != by_vector:
                continue
            c = 512 * (f + 4 * (q % 2))
            out, src = T.et[:, 4 * a + f:4 * b:4], T.z[:, c:c + 128]
            if by_vector:
                V.wait_ge(sem["z%d%d" % (f, q)], 1)
                V.tensor_copy(out, src).then_inc(sem["c%d" % q], 1)
            else:
                S.wait_ge(sem["z%d%d" % (f, q)], 1)
                S.activation(out, src, COPY).then_inc(sem["c%d" % q], 1)

    def make_e(q):
        copy(q, True)
        a, b = 128 * q, 128 * q + 128
        V.wait_ge(sem["c%d" % q], 4)
        V.quantize_mx(T.xc[:, a:b], T.xsc[:, a:b], T.et[:, 4 * a:4 * b]).then_inc(sem["e%d" % q], 1)

    make_o(0)
    V.wait_ge(sem.ltab, 16)
    for f in range(4):
        V.quantize_mx(T.tq[:, 128 * f:128 * f + 128], T.tqs[:, 128 * f:128 * f + 128],
                      T.tabs[:, 512 * f:512 * f + 512]).then_inc(sem.tqd, 1)
    V.wait_ge(sem.lw, 16)
    V.quantize_mx(T.wq[:], T.wqs[:], T.ws[:]).then_inc(sem.wqd, 1)
    for step in CFG["VSEQ"][rank]:
        (make_o if step[0] == "o" else make_e)(int(step[1]))
    spread(0, False)
    for step in CFG["SSEQ"][rank]:
        if step[0] == "x":
            spread(int(step[1]), False)
        else:
            copy(int(step[1]), False)
    for q in range(N):
        make_z(q)

    for step in CFG["SEND"][rank]:
        kind, dst = step[0], [int(d) for d in step[1:]]
        for j in dst:
            g.wait_ge(sem["e%d" % order.index(j)], 1)
        moves = []
        for j in dst:
            c, s, up = e_to(kind, rank, j)
            q = order.index(j)
            moves.append((c, codes(T.ec, s), codes(T.xc, q), up) if kind == "C" else
                         (c, planes(T.esc, s), planes(T.xsc, q), up))
        send(moves)

    E.wait_ge(sem.wqd, 1)
    E.wait_ge(sem.e0, 1)
    E.wait_ge(sem.c4, 4)
    far = [r for r in range(N) if (r, rank) in DIAG]
    near = [r for r in range(N) if r != rank and r not in far]
    E.matmul_mx(T.z[:, 0:128], T.wq[:], T.wqs[:], T.xc[:, 0:128], T.xsc[:, 0:128], True, False)
    todo = near + far
    for r in todo:
        p = 128 * POS[r]
        E.wait_ge(sem["cin%d" % r], e_in("C", r, rank))
        E.wait_ge(sem["sin%d" % r], e_in("S", r, rank))
        last = r == todo[-1]
        m = E.matmul_mx(T.z[:, 0:128], T.wq[:], T.wqs[:], T.ec[:, p:p + 128], T.esc[:, p:p + 128], False, last)
        if last:
            m.then_inc(sem.yd, 1)
    V.wait_ge(sem.yd, 1)
    V.tensor_copy(T.ysb[:], T.z[:, 0:128]).then_inc(sem.yc, 1)
    Y.wait_ge(sem.yc, 1)
    Y.dma_start(T.y[:, :], T.ysb[:]).then_inc(sem.yst, 16)
    Y.wait_ge(sem.yst, 16)
    g.wait_ge(sem.sent, sent[0])
